import numpy as np
CORES = [0,1,2,3,4,5,6,7]
N = 8
def setup_inputs(rng):
    return {"x": rng.standard_normal((N, 128, 4096), dtype=np.float32)}
def reference(x):
    s = x.max(axis=0)
    b = 4096 // N
    return {"y": np.stack([s[:, r * b:(r + 1) * b] for r in range(N)])}

@@ -1,0 +1,53 @@
+from concourse.bass import DstId, RemoteDMATransfer
+
+N = 8
+B = 4096 // N
+
+SCRATCH = {
+    "xs": ("sbuf", [128, 4096], "float32"),
+    "land": ("sbuf", [128, (N - 1) * B], "float32"),
+    "res": ("sbuf", [128, B], "float32"),
+}
+SEMAPHORES = ["ld%d" % k for k in range(N)] + ["arrived", "done", "sent", "stored"]
+
+
+def rank_program(g, core, T, topo):
+    r = T.rank_of(core)
+    if r is None:
+        return
+
+    def cols(j):
+        return slice(j * B, (j + 1) * B)
+
+    for k in range(N):
+        j = (r + k) % N
+        q = g.sync if k % 2 == 0 else g.scalar
+        q.dma_start(T.xs[:, cols(j)], T.x[:, cols(j)]).then_inc(T.sem["ld%d" % k], 16)
+
+    for k in range(N - 1):
+        j = (r + k) % N
+        h = (j + 1) % N
+        dst = T.cores[h]
+        rid, pid, _se = topo.addr(dst)
+        slot = (r - h - 1) % N
+        g.wait_ge(T.sem["ld%d" % k], 16)
+        g.remote_dma(T.land[:, cols(slot)], T.xs[:, cols(j)], T.sem.arrived, T.sem.sent,
+                     pid, rid, topo.mask(core, dst))
+
+    j = (r - 1) % N
+    dst = T.cores[j]
+    rid, pid, _se = topo.addr(dst)
+    g.wait_ge(T.sem["ld%d" % (N - 1)], 16)
+    g.wait_ge(T.sem.arrived, 16 * (N - 1))
+    g.remote_dma_fused(
+        [RemoteDMATransfer(dst_ids=[DstId(rid=rid, pnc=pid)], dma_engine_mask=topo.mask(core, dst),
+                           remote_sem=T.sem.done,
+                           srcs=[T.xs[:, cols(j)]] + [T.land[:, cols(s)] for s in range(N - 1)],
+                           dsts=[T.res[:]], alu_op=2)],
+        local_sem=T.sem.sent)
+
+    g.sync.wait_ge(T.sem.done, 16)
+    g.sync.dma_start(T.y[:], T.res[:]).then_inc(T.sem.stored, 16)
+    g.wait_ge(T.sem.done, 16)
+    g.wait_ge(T.sem.sent, 16 * N)
+    g.wait_ge(T.sem.stored, 16)

@@ -2,13 +2,14 @@ from concourse.bass import DstId, RemoteDMATransfer
 
 N = 8
 B = 4096 // N
+ORDER = [4, 1, 5, 2, 6, 3, 7]
 
 SCRATCH = {
     "xs": ("sbuf", [128, 4096], "float32"),
     "land": ("sbuf", [128, (N - 1) * B], "float32"),
     "res": ("sbuf", [128, B], "float32"),
 }
-SEMAPHORES = ["ld%d" % k for k in range(N)] + ["arrived", "done", "sent", "stored"]
+SEMAPHORES = ["ld%d" % i for i in range(N)] + ["arrived", "done", "sent", "stored"]
 
 
 def rank_program(g, core, T, topo):
@@ -19,30 +20,28 @@ def rank_program(g, core, T, topo):
     def cols(j):
         return slice(j * B, (j + 1) * B)
 
-    for k in range(N):
-        j = (r + k) % N
-        q = g.sync if k % 2 == 0 else g.scalar
-        q.dma_start(T.xs[:, cols(j)], T.x[:, cols(j)]).then_inc(T.sem["ld%d" % k], 16)
+    mine = r ^ 1
+    blocks = [r ^ k ^ 1 for k in ORDER] + [mine]
 
-    for k in range(N - 1):
-        j = (r + k) % N
-        h = (j + 1) % N
-        dst = T.cores[h]
+    for i, j in enumerate(blocks):
+        q = g.sync if i % 2 == 0 else g.scalar
+        q.dma_start(T.xs[:, cols(j)], T.x[:, cols(j)]).then_inc(T.sem["ld%d" % i], 16)
+
+    for i, k in enumerate(ORDER):
+        dst = T.cores[r ^ k]
         rid, pid, _se = topo.addr(dst)
-        slot = (r - h - 1) % N
-        g.wait_ge(T.sem["ld%d" % k], 16)
-        g.remote_dma(T.land[:, cols(slot)], T.xs[:, cols(j)], T.sem.arrived, T.sem.sent,
+        g.wait_ge(T.sem["ld%d" % i], 16)
+        g.remote_dma(T.land[:, cols(k - 1)], T.xs[:, cols(blocks[i])], T.sem.arrived, T.sem.sent,
                      pid, rid, topo.mask(core, dst))
 
-    j = (r - 1) % N
-    dst = T.cores[j]
+    dst = T.cores[mine]
     rid, pid, _se = topo.addr(dst)
     g.wait_ge(T.sem["ld%d" % (N - 1)], 16)
     g.wait_ge(T.sem.arrived, 16 * (N - 1))
     g.remote_dma_fused(
         [RemoteDMATransfer(dst_ids=[DstId(rid=rid, pnc=pid)], dma_engine_mask=topo.mask(core, dst),
                            remote_sem=T.sem.done,
-                           srcs=[T.xs[:, cols(j)]] + [T.land[:, cols(s)] for s in range(N - 1)],
+                           srcs=[T.xs[:, cols(mine)]] + [T.land[:, cols(s)] for s in range(N - 1)],
                            dsts=[T.res[:]], alu_op=2)],
         local_sem=T.sem.sent)
 

from concourse.bass import DstId, RemoteDMATransfer

N = 8
B = 4096 // N
ORDER = [4, 1, 5, 2, 6, 3, 7]

SCRATCH = {
    "xs": ("sbuf", [128, 4096], "float32"),
    "land": ("sbuf", [128, (N - 1) * B], "float32"),
    "res": ("sbuf", [128, B], "float32"),
}
SEMAPHORES = ["ld%d" % i for i in range(N)] + ["arrived", "done", "sent", "stored"]


def rank_program(g, core, T, topo):
    r = T.rank_of(core)
    if r is None:
        return

    def cols(j):
        return slice(j * B, (j + 1) * B)

    mine = r ^ 1
    blocks = [r ^ k ^ 1 for k in ORDER] + [mine]

    for i, j in enumerate(blocks):
        q = g.sync if i % 2 == 0 else g.scalar
        q.dma_start(T.xs[:, cols(j)], T.x[:, cols(j)]).then_inc(T.sem["ld%d" % i], 16)

    for i, k in enumerate(ORDER):
        dst = T.cores[r ^ k]
        rid, pid, _se = topo.addr(dst)
        g.wait_ge(T.sem["ld%d" % i], 16)
        g.remote_dma(T.land[:, cols(k - 1)], T.xs[:, cols(blocks[i])], T.sem.arrived, T.sem.sent,
                     pid, rid, topo.mask(core, dst))

    dst = T.cores[mine]
    rid, pid, _se = topo.addr(dst)
    g.wait_ge(T.sem["ld%d" % (N - 1)], 16)
    g.wait_ge(T.sem.arrived, 16 * (N - 1))
    g.remote_dma_fused(
        [RemoteDMATransfer(dst_ids=[DstId(rid=rid, pnc=pid)], dma_engine_mask=topo.mask(core, dst),
                           remote_sem=T.sem.done,
                           srcs=[T.xs[:, cols(mine)]] + [T.land[:, cols(s)] for s in range(N - 1)],
                           dsts=[T.res[:]], alu_op=2)],
        local_sem=T.sem.sent)

    g.sync.wait_ge(T.sem.done, 16)
    g.sync.dma_start(T.y[:], T.res[:]).then_inc(T.sem.stored, 16)
    g.wait_ge(T.sem.done, 16)
    g.wait_ge(T.sem.sent, 16 * N)
    g.wait_ge(T.sem.stored, 16)
